import numpy as np
import ml_dtypes


def mxq(x, axis, fmt="e4m3"):
    dtype, down = {"e4m3": (ml_dtypes.float8_e4m3fn, 7), "e5m2": (ml_dtypes.float8_e5m2, 14)}[fmt]
    v = np.moveaxis(np.asarray(x, np.float32).astype(ml_dtypes.bfloat16).astype(np.float64), axis, -1)
    blocks = v.reshape(v.shape[:-1] + (-1, 32))
    amax = np.abs(blocks).max(-1, keepdims=True)
    byte = np.maximum(np.where(amax > 0, np.frexp(amax)[1] - 1 + 127, 0) - down, 1)
    scale = np.exp2(byte - 127.0)
    codes = (blocks / scale).astype(np.float32).astype(dtype).astype(np.float64)
    return np.moveaxis((codes * scale).reshape(v.shape), -1, axis)


WIDE = False


def mx_kscale(k):
    if not WIDE:
        return np.ones(k)
    levels = np.array([30, -30])
    if k % 512:
        return np.exp2(np.random.permutation(np.resize(levels, k // 32))).repeat(32)
    a = np.empty((k // 512, 16))
    for p in range(k // 512):
        a[p, :8] = np.random.permutation(np.resize(levels, 8))
        for g in range(8):
            far = levels[np.abs(levels - a[p, g]) >= 10]
            a[p, g + 8] = far[np.random.randint(len(far))]
    return np.exp2(a.ravel()).repeat(32)


BF16 = ml_dtypes.bfloat16


def bf(x):
    return np.asarray(x, np.float32).astype(BF16)


def f64(x):
    return np.asarray(x).astype(np.float64)


E2M1 = np.array([0.0, 0.5, 1.0, 1.5, 2.0, 3.0, 4.0, 6.0, -0.0, -0.5, -1.0, -1.5, -2.0, -3.0, -4.0, -6.0])


def pack_weight(w, fmt):
    k, n = w.shape
    w = f64(bf(w)).reshape(k // 32, 32, n)
    amax = np.abs(w).max(1)
    if fmt in ("e4m3", "e5m2"):
        byte = np.frexp(amax)[1] - 1 + 127 - (7 if fmt == "e4m3" else 14)
    else:
        mant, ex = np.frexp(amax / 6.0)
        byte = np.where(mant > 0.5, ex, ex - 1) + 127
    byte = np.clip(np.where(amax > 0, byte, 1), 1, 254)
    scaled = (w * np.exp2(127.0 - byte)[:, None, :]).reshape(k, n).astype(np.float32)
    by_word = np.ascontiguousarray(scaled.reshape(k // 512, 128, 4, n).transpose(0, 1, 3, 2))
    if fmt in ("e4m3", "e5m2"):
        words = by_word.astype(ml_dtypes.float8_e4m3fn if fmt == "e4m3" else ml_dtypes.float8_e5m2).view(np.uint8)
    else:
        c = by_word.astype(ml_dtypes.float4_e2m1fn).view(np.uint8) & 0xF
        words = c[..., 0::2] | (c[..., 1::2] << 4)
    return np.ascontiguousarray(words), np.ascontiguousarray(byte.astype(np.uint8).reshape(k // 512, 16, n))


def unpack_weight(words, scales, fmt):
    g, p, n, _ = words.shape
    if fmt in ("e4m3", "e5m2"):
        vals = np.ascontiguousarray(words).view(ml_dtypes.float8_e4m3fn if fmt == "e4m3" else ml_dtypes.float8_e5m2).astype(np.float64)
    else:
        nib = np.empty((g, p, n, 4), np.uint8)
        nib[..., 0::2] = words & 0xF
        nib[..., 1::2] = words >> 4
        vals = E2M1[nib]
    vals = vals * np.repeat(np.exp2(scales.astype(np.float64) - 127.0), 8, axis=1)[..., None]
    return vals.transpose(0, 1, 3, 2).reshape(g * 512, n)


T, F, V, ND, NC = 4096, 512, 128, 512, 1024


def setup_inputs():
    s = mx_kscale(T)[:, None]
    D = np.random.standard_normal((T, ND)) * np.exp(np.random.standard_normal((T, 1)) - 1) / np.sqrt(T) / s
    C = np.random.standard_normal((T, NC)) * np.exp(np.random.standard_normal((T, 1)) - 1) / np.sqrt(T) / s
    d_words, d_scales = pack_weight(D, "e5m2")
    c_words, c_scales = pack_weight(C, "e5m2")
    return {"x": bf(np.random.standard_normal((T, F)) * s),
            "dirs": bf(np.random.standard_normal((T, V)) * s),
            "gate": bf(1 + 0.1 * np.random.standard_normal(F)),
            "d_words": d_words, "d_scales": d_scales,
            "c_words": c_words, "c_scales": c_scales,
            "acc_d": bf(np.random.standard_normal((F, ND))),
            "acc_x": bf(np.random.standard_normal((F, NC))),
            "acc_v": bf(np.random.standard_normal((V, NC)))}


def reference(x, dirs, gate, d_words, d_scales, c_words, c_scales, acc_d, acc_x, acc_v):
    D = unpack_weight(d_words, d_scales, "e5m2")
    C = unpack_weight(c_words, c_scales, "e5m2")
    xq = mxq(f64(x), 0, "e4m3")
    vq = mxq(f64(dirs), 0, "e4m3")
    grad_d = f64(acc_d) + (xq.T @ D)
    grad_x = f64(acc_x) + f64(gate)[:, None] * (xq.T @ C)
    grad_v = f64(acc_v) + (vq.T @ C)
    return grad_d, grad_x, grad_v

@@ -1,0 +1,205 @@
+from contextlib import ExitStack
+
+import concourse.mybir as mybir
+
+T, F, V, ND, NC = 4096, 512, 128, 512, 1024
+FLOPS = 2 * T * (F * ND + F * NC + V * NC)
+
+F32 = mybir.dt.float32
+BF16 = mybir.dt.bfloat16
+I32 = mybir.dt.int32
+U32 = mybir.dt.uint32
+U8 = mybir.dt.uint8
+E4M3 = mybir.dt.float8_e4m3fn_x4
+E5M2 = mybir.dt.float8_e5m2_x4
+MULT = mybir.AluOpType.mult
+ADD = mybir.AluOpType.add
+
+P = 128
+PACK = 4
+PASSES = T // (P * PACK)
+JB = F // P
+NT = 512
+EARLY = 2
+
+
+def tile_radiance_branch_weight_gradients_e2_kernel(
+    tc, x, dirs, gate, d_words, d_scales, c_words, c_scales, acc_d, acc_x, acc_v, out_d, out_x, out_v
+):
+    nc = tc.nc
+
+    x_v = x.rearrange("(g p t) f -> p g (t f)", p=P, t=PACK)
+    dirs_v = dirs.rearrange("(g p t) v -> p g (t v)", p=P, t=PACK)
+    c_v = c_words.rearrange("g p n t -> p g (n t)").bitcast(I32)
+    d_v = d_words.rearrange("g p n t -> p g (n t)").bitcast(I32)
+    cs_v = c_scales.rearrange("g q n -> q g n").bitcast(I32)
+    ds_v = d_scales.rearrange("g q n -> q g n").bitcast(I32)
+    acc_x_v = acc_x.rearrange("(m j) n -> m j n", j=JB)
+    acc_d_v = acc_d.rearrange("(m j) n -> m j n", j=JB)
+    out_x_v = out_x.rearrange("(m j) n -> m j n", j=JB)
+    out_d_v = out_d.rearrange("(m j) n -> m j n", j=JB)
+    gate_v = gate.rearrange("(m j) -> m j", j=JB)
+
+    with ExitStack() as ctx:
+        keep = ctx.enter_context(tc.tile_pool(name="keep", bufs=1))
+        stage = ctx.enter_context(tc.tile_pool(name="stage", bufs=3))
+        psum = ctx.enter_context(tc.psum_pool(name="psum", bufs=1))
+
+        x_raw = keep.tile([P, PASSES, PACK * F], BF16, align_bytes=64)
+        x_codes = keep.tile([P, PASSES, F], U32, align_bytes=64)
+        x_scales = keep.tile([P, PASSES, F], U8, align_bytes=64)
+        v_raw = keep.tile([P, PASSES, PACK * V], BF16, align_bytes=64)
+        v_codes = keep.tile([P, PASSES, V], U32, align_bytes=64)
+        v_scales = keep.tile([P, PASSES, V], U8, align_bytes=64)
+        c_codes = keep.tile([P, PASSES, NC], U32, align_bytes=64)
+        d_codes = keep.tile([P, PASSES, ND], U32, align_bytes=64)
+        cs_early = keep.tile([P, EARLY, NC], U8, align_bytes=64)
+        cs_late = keep.tile([P, PASSES - EARLY, NC], U8, align_bytes=64)
+        ds = keep.tile([P, PASSES, ND], U8, align_bytes=64)
+        ax = keep.tile([P, JB, NC], BF16, align_bytes=64)
+        ad = keep.tile([P, JB, ND], BF16, align_bytes=64)
+        av = keep.tile([P, NC], BF16, align_bytes=64)
+        gate_sb = keep.tile([P, JB], BF16, align_bytes=64)
+        ox = keep.tile([P, JB, NC], F32, align_bytes=64)
+        od = keep.tile([P, JB, ND], F32, align_bytes=64)
+        ov = keep.tile([P, NC], F32, align_bytes=64)
+
+        ctx.enter_context(tc.manual_schedule())
+
+        nc.vector.memset(cs_early[:].rearrange("p g n -> p (g n)").bitcast(I32), 0)
+        nc.vector.memset(cs_late[:].rearrange("p g n -> p (g n)").bitcast(I32), 0)
+        nc.gpsimd.memset(ds[:].rearrange("p g n -> p (g n)").bitcast(I32), 0)
+        for q in range(4):
+            nc.scalar.dma_start(
+                out=cs_early[32 * q : 32 * q + 4, :, :].bitcast(I32), in_=cs_v[4 * q : 4 * q + 4, 0:EARLY, :]
+            )
+        for q in range(4):
+            nc.gpsimd.dma_start(
+                out=cs_late[32 * q : 32 * q + 4, :, :].bitcast(I32), in_=cs_v[4 * q : 4 * q + 4, EARLY:PASSES, :]
+            )
+        for q in range(4):
+            nc.gpsimd.dma_start(out=ds[32 * q : 32 * q + 4, :, :].bitcast(I32), in_=ds_v[4 * q : 4 * q + 4, :, :])
+        nc.gpsimd.dma_start(out=gate_sb[:], in_=gate_v)
+
+        for s in range(PASSES):
+            nc.sync.dma_start(out=x_raw[:, s, :], in_=x_v[:, s, :])
+            nc.sync.dma_start(out=c_codes[:, s, :].bitcast(I32), in_=c_v[:, s, :])
+
+        def load_d(s0, s1):
+            nc.sync.dma_start(out=d_codes[:, s0:s1, :].bitcast(I32), in_=d_v[:, s0:s1, :])
+
+        def load_dirs(s0, s1):
+            nc.sync.dma_start(out=v_raw[:, s0:s1, :], in_=dirs_v[:, s0:s1, :])
+
+        nc.sync.dma_start(out=ax[:], in_=acc_x_v)
+        load_d(0, 1)
+        load_d(1, 2)
+        load_d(2, 4)
+        load_dirs(0, 4)
+        load_d(4, 6)
+        load_dirs(4, 8)
+        load_d(6, 8)
+        nc.sync.dma_start(out=ad[:], in_=acc_d_v)
+        nc.sync.dma_start(out=av[:], in_=acc_v)
+
+        def matmul(bank, codes, scales, rhs, rhs_scale, s):
+            nc.tensor.matmul_mx(
+                out=bank[:],
+                lhsT=codes.bitcast(E4M3),
+                lhsT_scale=scales,
+                rhs=rhs.bitcast(E5M2),
+                rhs_scale=rhs_scale,
+                start=(s == 0),
+                stop=(s == PASSES - 1),
+            )
+
+        def c_scale(s, n0):
+            if s < EARLY:
+                return cs_early[:, s, n0 : n0 + NT]
+            return cs_late[:, s - EARLY, n0 : n0 + NT]
+
+        x_banks = []
+        for i in range(8):
+            bank = psum.tile([P, NT], F32, name="bank%d" % i)
+            x_banks.append(bank)
+        H = JB // 2
+        for s in range(PASSES):
+            grouped = stage.tile([P, JB, P, PACK], BF16, align_bytes=64)
+            raw = x_raw[:, s, :].rearrange("p (t m j) -> p j m t", t=PACK, j=JB)
+            nc.scalar.copy(out=grouped[:, H:JB, :, :], in_=raw[:, H:JB, :, :])
+            nc.vector.tensor_copy(out=grouped[:, 0:H, :, :], in_=raw[:, 0:H, :, :])
+            for h in range(2):
+                cols = slice(h * H * P, (h + 1) * H * P)
+                nc.vector.quantize_mx(
+                    out=x_codes[:, s, cols].bitcast(E4M3),
+                    scales=x_scales[:, s, cols],
+                    in_=grouped[:, h * H : (h + 1) * H, :, :].rearrange("p j m t -> p (j m t)"),
+                )
+            for j in range(JB):
+                for nh in range(2):
+                    n0 = nh * NT
+                    matmul(
+                        x_banks[2 * j + nh],
+                        x_codes[:, s, P * j : P * (j + 1)],
+                        x_scales[:, s, P * j : P * (j + 1)],
+                        c_codes[:, s, n0 : n0 + NT],
+                        c_scale(s, n0),
+                        s,
+                    )
+
+        for j in range(JB):
+            for nh in range(2):
+                n0 = nh * NT
+                nc.vector.scalar_tensor_tensor(
+                    out=ox[:, j, n0 : n0 + NT],
+                    in0=x_banks[2 * j + nh][:],
+                    scalar=gate_sb[:, j : j + 1],
+                    in1=ax[:, j, n0 : n0 + NT],
+                    op0=MULT,
+                    op1=ADD,
+                )
+            if j % 2 == 1:
+                nc.sync.dma_start(out=out_x_v[:, j - 1 : j + 1, :], in_=ox[:, j - 1 : j + 1, :])
+
+        d_banks = []
+        for i in range(JB):
+            bank = psum.tile([P, NT], F32, name="bank%d" % i)
+            d_banks.append(bank)
+        for s in range(PASSES):
+            for j in range(JB):
+                matmul(
+                    d_banks[j],
+                    x_codes[:, s, P * j : P * (j + 1)],
+                    x_scales[:, s, P * j : P * (j + 1)],
+                    d_codes[:, s, :],
+                    ds[:, s, :],
+                    s,
+                )
+
+        HP = PASSES // 2
+        for h in range(2):
+            v_grouped = stage.tile([P, HP, V, PACK], BF16, align_bytes=64)
+            s0, s1 = h * HP, (h + 1) * HP
+            raw = v_raw[:, s0:s1, :].rearrange("p s (t c) -> p s c t", t=PACK)
+            if h == 0:
+                nc.scalar.copy(out=v_grouped[:], in_=raw)
+            else:
+                nc.vector.tensor_copy(out=v_grouped[:], in_=raw)
+            nc.vector.quantize_mx(
+                out=v_codes[:, s0:s1, :].rearrange("p s c -> p (s c)").bitcast(E4M3),
+                scales=v_scales[:, s0:s1, :].rearrange("p s c -> p (s c)"),
+                in_=v_grouped[:].rearrange("p s c t -> p (s c t)"),
+            )
+
+        for j in range(JB):
+            nc.vector.tensor_tensor(out=od[:, j, :], in0=d_banks[j][:], in1=ad[:, j, :], op=ADD)
+            if j % 2 == 1:
+                nc.sync.dma_start(out=out_d_v[:, j - 1 : j + 1, :], in_=od[:, j - 1 : j + 1, :])
+
+        for nh in range(2):
+            n0 = nh * NT
+            bank = psum.tile([P, NT], F32, name="bank%d" % (JB + nh))
+            for s in range(PASSES):
+                matmul(bank, v_codes[:, s, :], v_scales[:, s, :], c_codes[:, s, n0 : n0 + NT], c_scale(s, n0), s)
+            nc.vector.tensor_tensor(out=ov[:, n0 : n0 + NT], in0=bank[:], in1=av[:, n0 : n0 + NT], op=ADD)
+            nc.sync.dma_start(out=out_v[:, n0 : n0 + NT], in_=ov[:, n0 : n0 + NT])

@@ -34,11 +34,11 @@ def tile_radiance_branch_weight_gradients_e2_kernel(
     d_v = d_words.rearrange("g p n t -> p g (n t)").bitcast(I32)
     cs_v = c_scales.rearrange("g q n -> q g n").bitcast(I32)
     ds_v = d_scales.rearrange("g q n -> q g n").bitcast(I32)
-    acc_x_v = acc_x.rearrange("(m j) n -> m j n", j=JB)
-    acc_d_v = acc_d.rearrange("(m j) n -> m j n", j=JB)
-    out_x_v = out_x.rearrange("(m j) n -> m j n", j=JB)
-    out_d_v = out_d.rearrange("(m j) n -> m j n", j=JB)
-    gate_v = gate.rearrange("(m j) -> m j", j=JB)
+    acc_x_v = acc_x.rearrange("(j m) n -> m j n", j=JB)
+    acc_d_v = acc_d.rearrange("(j m) n -> m j n", j=JB)
+    out_x_v = out_x.rearrange("(j m) n -> m j n", j=JB)
+    out_d_v = out_d.rearrange("(j m) n -> m j n", j=JB)
+    gate_v = gate.rearrange("(j m o) -> m j o", j=JB, o=1)
 
     with ExitStack() as ctx:
         keep = ctx.enter_context(tc.tile_pool(name="keep", bufs=1))
@@ -59,7 +59,7 @@ def tile_radiance_branch_weight_gradients_e2_kernel(
         ax = keep.tile([P, JB, NC], BF16, align_bytes=64)
         ad = keep.tile([P, JB, ND], BF16, align_bytes=64)
         av = keep.tile([P, NC], BF16, align_bytes=64)
-        gate_sb = keep.tile([P, JB], BF16, align_bytes=64)
+        gate_sb = keep.tile([P, JB, 2], BF16, align_bytes=64)
         ox = keep.tile([P, JB, NC], F32, align_bytes=64)
         od = keep.tile([P, JB, ND], F32, align_bytes=64)
         ov = keep.tile([P, NC], F32, align_bytes=64)
@@ -68,7 +68,7 @@ def tile_radiance_branch_weight_gradients_e2_kernel(
 
         nc.vector.memset(cs_early[:].rearrange("p g n -> p (g n)").bitcast(I32), 0)
         nc.vector.memset(cs_late[:].rearrange("p g n -> p (g n)").bitcast(I32), 0)
-        nc.gpsimd.memset(ds[:].rearrange("p g n -> p (g n)").bitcast(I32), 0)
+        nc.vector.memset(ds[:].rearrange("p g n -> p (g n)").bitcast(I32), 0)
         for q in range(4):
             nc.scalar.dma_start(
                 out=cs_early[32 * q : 32 * q + 4, :, :].bitcast(I32), in_=cs_v[4 * q : 4 * q + 4, 0:EARLY, :]
@@ -79,7 +79,8 @@ def tile_radiance_branch_weight_gradients_e2_kernel(
             )
         for q in range(4):
             nc.gpsimd.dma_start(out=ds[32 * q : 32 * q + 4, :, :].bitcast(I32), in_=ds_v[4 * q : 4 * q + 4, :, :])
-        nc.gpsimd.dma_start(out=gate_sb[:], in_=gate_v)
+        with nc.allow_non_contiguous_dma(reason="one factor to a feature"):
+            nc.scalar.dma_start(out=gate_sb[:, :, 0:1], in_=gate_v)
 
         for s in range(PASSES):
             nc.sync.dma_start(out=x_raw[:, s, :], in_=x_v[:, s, :])
@@ -125,15 +126,17 @@ def tile_radiance_branch_weight_gradients_e2_kernel(
         H = JB // 2
         for s in range(PASSES):
             grouped = stage.tile([P, JB, P, PACK], BF16, align_bytes=64)
-            raw = x_raw[:, s, :].rearrange("p (t m j) -> p j m t", t=PACK, j=JB)
-            nc.scalar.copy(out=grouped[:, H:JB, :, :], in_=raw[:, H:JB, :, :])
-            nc.vector.tensor_copy(out=grouped[:, 0:H, :, :], in_=raw[:, 0:H, :, :])
-            for h in range(2):
-                cols = slice(h * H * P, (h + 1) * H * P)
+            raw = x_raw[:, s, :].rearrange("p (t j m) -> p j m t", t=PACK, j=JB)
+            w = 1 if s == 0 else 2
+            for b in range(0, H, w):
+                nc.scalar.copy(out=grouped[:, H + b : H + b + w, :, :], in_=raw[:, H + b : H + b + w, :, :])
+                nc.vector.tensor_copy(out=grouped[:, b : b + w, :, :], in_=raw[:, b : b + w, :, :])
+            for b in range(0, JB, w):
+                cols = slice(b * P, (b + w) * P)
                 nc.vector.quantize_mx(
                     out=x_codes[:, s, cols].bitcast(E4M3),
                     scales=x_scales[:, s, cols],
-                    in_=grouped[:, h * H : (h + 1) * H, :, :].rearrange("p j m t -> p (j m t)"),
+                    in_=grouped[:, b : b + w, :, :].rearrange("p j m t -> p (j m t)"),
                 )
             for j in range(JB):
                 for nh in range(2):
@@ -153,7 +156,7 @@ def tile_radiance_branch_weight_gradients_e2_kernel(
                 nc.vector.scalar_tensor_tensor(
                     out=ox[:, j, n0 : n0 + NT],
                     in0=x_banks[2 * j + nh][:],
-                    scalar=gate_sb[:, j : j + 1],
+                    scalar=gate_sb[:, j, 0:1],
                     in1=ax[:, j, n0 : n0 + NT],
                     op0=MULT,
                     op1=ADD,

@@ -21,6 +21,7 @@ PASSES = T // (P * PACK)
 JB = F // P
 NT = 512
 EARLY = 2
+HP = PASSES // 2
 
 
 def tile_radiance_branch_weight_gradients_e2_kernel(
@@ -54,36 +55,48 @@ def tile_radiance_branch_weight_gradients_e2_kernel(
         c_codes = keep.tile([P, PASSES, NC], U32, align_bytes=64)
         d_codes = keep.tile([P, PASSES, ND], U32, align_bytes=64)
         cs_early = keep.tile([P, EARLY, NC], U8, align_bytes=64)
-        cs_late = keep.tile([P, PASSES - EARLY, NC], U8, align_bytes=64)
-        ds = keep.tile([P, PASSES, ND], U8, align_bytes=64)
+        cs_mid = keep.tile([P, HP - EARLY, NC], U8, align_bytes=64)
+        cs_late = keep.tile([P, HP, NC], U8, align_bytes=64)
+        ds_early = keep.tile([P, HP, ND], U8, align_bytes=64)
+        ds_late = keep.tile([P, HP, ND], U8, align_bytes=64)
         ax = keep.tile([P, JB, NC], BF16, align_bytes=64)
         ad = keep.tile([P, JB, ND], BF16, align_bytes=64)
         av = keep.tile([P, NC], BF16, align_bytes=64)
         gate_sb = keep.tile([P, JB, 2], BF16, align_bytes=64)
+        gate_f = keep.tile([P, JB], F32, align_bytes=64)
         ox = keep.tile([P, JB, NC], F32, align_bytes=64)
         od = keep.tile([P, JB, ND], F32, align_bytes=64)
         ov = keep.tile([P, NC], F32, align_bytes=64)
 
         ctx.enter_context(tc.manual_schedule())
 
-        nc.vector.memset(cs_early[:].rearrange("p g n -> p (g n)").bitcast(I32), 0)
+        nc.gpsimd.memset(cs_early[:].rearrange("p g n -> p (g n)").bitcast(I32), 0)
+        nc.vector.memset(cs_mid[:].rearrange("p g n -> p (g n)").bitcast(I32), 0)
         nc.vector.memset(cs_late[:].rearrange("p g n -> p (g n)").bitcast(I32), 0)
-        nc.vector.memset(ds[:].rearrange("p g n -> p (g n)").bitcast(I32), 0)
+        nc.vector.memset(ds_early[:].rearrange("p g n -> p (g n)").bitcast(I32), 0)
+        nc.vector.memset(ds_late[:].rearrange("p g n -> p (g n)").bitcast(I32), 0)
         for q in range(4):
             nc.scalar.dma_start(
                 out=cs_early[32 * q : 32 * q + 4, :, :].bitcast(I32), in_=cs_v[4 * q : 4 * q + 4, 0:EARLY, :]
             )
         for q in range(4):
             nc.gpsimd.dma_start(
-                out=cs_late[32 * q : 32 * q + 4, :, :].bitcast(I32), in_=cs_v[4 * q : 4 * q + 4, EARLY:PASSES, :]
+                out=cs_late[32 * q : 32 * q + 4, :, :].bitcast(I32), in_=cs_v[4 * q : 4 * q + 4, HP:PASSES, :]
             )
         for q in range(4):
-            nc.gpsimd.dma_start(out=ds[32 * q : 32 * q + 4, :, :].bitcast(I32), in_=ds_v[4 * q : 4 * q + 4, :, :])
+            nc.gpsimd.dma_start(
+                out=ds_late[32 * q : 32 * q + 4, :, :].bitcast(I32), in_=ds_v[4 * q : 4 * q + 4, HP:PASSES, :]
+            )
         with nc.allow_non_contiguous_dma(reason="one factor to a feature"):
             nc.scalar.dma_start(out=gate_sb[:, :, 0:1], in_=gate_v)
 
-        for s in range(PASSES):
+        def load_xc(s):
             nc.sync.dma_start(out=x_raw[:, s, :], in_=x_v[:, s, :])
+            if s == 1:
+                for q in range(4):
+                    nc.sync.dma_start(
+                        out=cs_mid[32 * q : 32 * q + 4, :, :].bitcast(I32), in_=cs_v[4 * q : 4 * q + 4, EARLY:HP, :]
+                    )
             nc.sync.dma_start(out=c_codes[:, s, :].bitcast(I32), in_=c_v[:, s, :])
 
         def load_d(s0, s1):
@@ -92,39 +105,52 @@ def tile_radiance_branch_weight_gradients_e2_kernel(
         def load_dirs(s0, s1):
             nc.sync.dma_start(out=v_raw[:, s0:s1, :], in_=dirs_v[:, s0:s1, :])
 
-        nc.sync.dma_start(out=ax[:], in_=acc_x_v)
-        load_d(0, 1)
-        load_d(1, 2)
+        for s in range(HP):
+            load_xc(s)
+        for q in range(4):
+            nc.sync.dma_start(
+                out=ds_early[32 * q : 32 * q + 4, :, :].bitcast(I32), in_=ds_v[4 * q : 4 * q + 4, 0:HP, :]
+            )
+        load_d(0, 2)
         load_d(2, 4)
+        nc.sync.dma_start(out=ax[:], in_=acc_x_v)
+        for s in range(HP, PASSES):
+            load_xc(s)
         load_dirs(0, 4)
         load_d(4, 6)
-        load_dirs(4, 8)
         load_d(6, 8)
+        load_dirs(4, 8)
         nc.sync.dma_start(out=ad[:], in_=acc_d_v)
         nc.sync.dma_start(out=av[:], in_=acc_v)
 
-        def matmul(bank, codes, scales, rhs, rhs_scale, s):
+        def matmul(bank, codes, scales, rhs, rhs_scale, start, stop):
             nc.tensor.matmul_mx(
                 out=bank[:],
                 lhsT=codes.bitcast(E4M3),
                 lhsT_scale=scales,
                 rhs=rhs.bitcast(E5M2),
                 rhs_scale=rhs_scale,
-                start=(s == 0),
-                stop=(s == PASSES - 1),
+                start=start,
+                stop=stop,
             )
 
         def c_scale(s, n0):
             if s < EARLY:
                 return cs_early[:, s, n0 : n0 + NT]
-            return cs_late[:, s - EARLY, n0 : n0 + NT]
+            if s < HP:
+                return cs_mid[:, s - EARLY, n0 : n0 + NT]
+            return cs_late[:, s - HP, n0 : n0 + NT]
 
-        x_banks = []
-        for i in range(8):
-            bank = psum.tile([P, NT], F32, name="bank%d" % i)
-            x_banks.append(bank)
+        def open_banks(numbers):
+            banks = []
+            for i in numbers:
+                bank = psum.tile([P, NT], F32, name="bank%d" % i)
+                banks.append(bank)
+            return banks
+
         H = JB // 2
-        for s in range(PASSES):
+
+        def quantize_x(s):
             grouped = stage.tile([P, JB, P, PACK], BF16, align_bytes=64)
             raw = x_raw[:, s, :].rearrange("p (t j m) -> p j m t", t=PACK, j=JB)
             w = 1 if s == 0 else 2
@@ -138,71 +164,114 @@ def tile_radiance_branch_weight_gradients_e2_kernel(
                     scales=x_scales[:, s, cols],
                     in_=grouped[:, b : b + w, :, :].rearrange("p j m t -> p (j m t)"),
                 )
+
+        def x_times_c(s, banks, start, stop):
             for j in range(JB):
                 for nh in range(2):
                     n0 = nh * NT
                     matmul(
-                        x_banks[2 * j + nh],
+                        banks[2 * j + nh],
                         x_codes[:, s, P * j : P * (j + 1)],
                         x_scales[:, s, P * j : P * (j + 1)],
                         c_codes[:, s, n0 : n0 + NT],
                         c_scale(s, n0),
-                        s,
+                        start,
+                        stop,
                     )
 
-        for j in range(JB):
-            for nh in range(2):
-                n0 = nh * NT
-                nc.vector.scalar_tensor_tensor(
-                    out=ox[:, j, n0 : n0 + NT],
-                    in0=x_banks[2 * j + nh][:],
-                    scalar=gate_sb[:, j, 0:1],
-                    in1=ax[:, j, n0 : n0 + NT],
-                    op0=MULT,
-                    op1=ADD,
-                )
-            if j % 2 == 1:
-                nc.sync.dma_start(out=out_x_v[:, j - 1 : j + 1, :], in_=ox[:, j - 1 : j + 1, :])
-
-        d_banks = []
-        for i in range(JB):
-            bank = psum.tile([P, NT], F32, name="bank%d" % i)
-            d_banks.append(bank)
-        for s in range(PASSES):
-            for j in range(JB):
+        def x_times_d(j, bank, passes):
+            for s in passes:
                 matmul(
-                    d_banks[j],
+                    bank,
                     x_codes[:, s, P * j : P * (j + 1)],
                     x_scales[:, s, P * j : P * (j + 1)],
                     d_codes[:, s, :],
-                    ds[:, s, :],
-                    s,
+                    ds_early[:, s, :] if s < HP else ds_late[:, s - HP, :],
+                    s == passes[0],
+                    s == passes[-1],
                 )
 
-        HP = PASSES // 2
+        def add_xc(banks, addend, blocks, store):
+            for j in blocks:
+                for nh in range(2):
+                    n0 = nh * NT
+                    nc.vector.scalar_tensor_tensor(
+                        out=ox[:, j, n0 : n0 + NT],
+                        in0=banks[2 * j + nh][:],
+                        scalar=gate_f[:, j : j + 1],
+                        in1=addend[:, j, n0 : n0 + NT],
+                        op0=MULT,
+                        op1=ADD,
+                    )
+                if store and j % 2 == 1:
+                    nc.sync.dma_start(out=out_x_v[:, j - 1 : j + 1, :], in_=ox[:, j - 1 : j + 1, :])
+
+        xc = open_banks([0, 1, 2, 3, 4, 5, 6, 7])
+        for s in range(HP):
+            quantize_x(s)
+            x_times_c(s, xc, s == 0, s == HP - 1)
+        nc.vector.tensor_copy(out=gate_f[:], in_=gate_sb[:, :, 0])
+        add_xc(xc, ax, range(H, JB), False)
+        for j in range(H):
+            for nh in range(2):
+                nc.scalar.activation(
+                    out=ox[:, j, nh * NT : (nh + 1) * NT],
+                    in_=xc[2 * j + nh][:],
+                    func=mybir.ActivationFunctionType.Copy,
+                    scale=gate_f[:, j : j + 1],
+                )
+        xd = open_banks([0, 1, 2, 3])
+        for j in range(JB):
+            x_times_d(j, xd[j], range(0, HP))
+
+        xc = open_banks([4, 5, 6, 7, 0, 1, 2, 3])
+        for s in range(HP, PASSES):
+            quantize_x(s)
+            if s == HP:
+                for j in range(JB):
+                    nc.scalar.copy(out=od[:, j, :], in_=xd[j][:])
+            j = s - HP - 1
+            if 0 <= j < H:
+                nc.vector.tensor_tensor(out=ox[:, j, :], in0=ox[:, j, :], in1=ax[:, j, :], op=ADD)
+            x_times_c(s, xc, s == HP, s == PASSES - 1)
+        add_xc(xc, ox, range(JB), True)
+        xd = open_banks([4, 5, 6, 7])
+        for j in range(JB):
+            x_times_d(j, xd[j], range(HP, PASSES))
+
         for h in range(2):
             v_grouped = stage.tile([P, HP, V, PACK], BF16, align_bytes=64)
             s0, s1 = h * HP, (h + 1) * HP
-            raw = v_raw[:, s0:s1, :].rearrange("p s (t c) -> p s c t", t=PACK)
-            if h == 0:
-                nc.scalar.copy(out=v_grouped[:], in_=raw)
-            else:
-                nc.vector.tensor_copy(out=v_grouped[:], in_=raw)
+            nc.scalar.copy(out=v_grouped[:], in_=v_raw[:, s0:s1, :].rearrange("p s (t c) -> p s c t", t=PACK))
             nc.vector.quantize_mx(
                 out=v_codes[:, s0:s1, :].rearrange("p s c -> p (s c)").bitcast(E4M3),
                 scales=v_scales[:, s0:s1, :].rearrange("p s c -> p (s c)"),
                 in_=v_grouped[:].rearrange("p s c t -> p (s c t)"),
             )
+            for j in range(2 * h, 2 * h + 2):
+                nc.vector.tensor_tensor(out=od[:, j, :], in0=od[:, j, :], in1=ad[:, j, :], op=ADD)
 
         for j in range(JB):
-            nc.vector.tensor_tensor(out=od[:, j, :], in0=d_banks[j][:], in1=ad[:, j, :], op=ADD)
+            nc.vector.tensor_tensor(out=od[:, j, :], in0=xd[j][:], in1=od[:, j, :], op=ADD)
             if j % 2 == 1:
                 nc.sync.dma_start(out=out_d_v[:, j - 1 : j + 1, :], in_=od[:, j - 1 : j + 1, :])
 
         for nh in range(2):
             n0 = nh * NT
-            bank = psum.tile([P, NT], F32, name="bank%d" % (JB + nh))
+            bank = open_banks([nh])[0]
             for s in range(PASSES):
-                matmul(bank, v_codes[:, s, :], v_scales[:, s, :], c_codes[:, s, n0 : n0 + NT], c_scale(s, n0), s)
-            nc.vector.tensor_tensor(out=ov[:, n0 : n0 + NT], in0=bank[:], in1=av[:, n0 : n0 + NT], op=ADD)
-            nc.sync.dma_start(out=out_v[:, n0 : n0 + NT], in_=ov[:, n0 : n0 + NT])
+                matmul(
+                    bank,
+                    v_codes[:, s, :],
+                    v_scales[:, s, :],
+                    c_codes[:, s, n0 : n0 + NT],
+                    c_scale(s, n0),
+                    s == 0,
+                    s == PASSES - 1,
+                )
+            pieces = 1 + nh
+            w = NT // pieces
+            for i in range(pieces):
+                cols = slice(n0 + i * w, n0 + (i + 1) * w)
+                nc.vector.tensor_tensor(out=ov[:, cols], in0=bank[:, i * w : (i + 1) * w], in1=av[:, cols], op=ADD)
+                nc.sync.dma_start(out=out_v[:, cols], in_=ov[:, cols])

from contextlib import ExitStack

import concourse.mybir as mybir

T, F, V, ND, NC = 4096, 512, 128, 512, 1024
FLOPS = 2 * T * (F * ND + F * NC + V * NC)

F32 = mybir.dt.float32
BF16 = mybir.dt.bfloat16
I32 = mybir.dt.int32
U32 = mybir.dt.uint32
U8 = mybir.dt.uint8
E4M3 = mybir.dt.float8_e4m3fn_x4
E5M2 = mybir.dt.float8_e5m2_x4
MULT = mybir.AluOpType.mult
ADD = mybir.AluOpType.add

P = 128
PACK = 4
PASSES = T // (P * PACK)
JB = F // P
NT = 512
EARLY = 2
HP = PASSES // 2


def tile_radiance_branch_weight_gradients_e2_kernel(
    tc, x, dirs, gate, d_words, d_scales, c_words, c_scales, acc_d, acc_x, acc_v, out_d, out_x, out_v
):
    nc = tc.nc

    x_v = x.rearrange("(g p t) f -> p g (t f)", p=P, t=PACK)
    dirs_v = dirs.rearrange("(g p t) v -> p g (t v)", p=P, t=PACK)
    c_v = c_words.rearrange("g p n t -> p g (n t)").bitcast(I32)
    d_v = d_words.rearrange("g p n t -> p g (n t)").bitcast(I32)
    cs_v = c_scales.rearrange("g q n -> q g n").bitcast(I32)
    ds_v = d_scales.rearrange("g q n -> q g n").bitcast(I32)
    acc_x_v = acc_x.rearrange("(j m) n -> m j n", j=JB)
    acc_d_v = acc_d.rearrange("(j m) n -> m j n", j=JB)
    out_x_v = out_x.rearrange("(j m) n -> m j n", j=JB)
    out_d_v = out_d.rearrange("(j m) n -> m j n", j=JB)
    gate_v = gate.rearrange("(j m o) -> m j o", j=JB, o=1)

    with ExitStack() as ctx:
        keep = ctx.enter_context(tc.tile_pool(name="keep", bufs=1))
        stage = ctx.enter_context(tc.tile_pool(name="stage", bufs=3))
        psum = ctx.enter_context(tc.psum_pool(name="psum", bufs=1))

        x_raw = keep.tile([P, PASSES, PACK * F], BF16, align_bytes=64)
        x_codes = keep.tile([P, PASSES, F], U32, align_bytes=64)
        x_scales = keep.tile([P, PASSES, F], U8, align_bytes=64)
        v_raw = keep.tile([P, PASSES, PACK * V], BF16, align_bytes=64)
        v_codes = keep.tile([P, PASSES, V], U32, align_bytes=64)
        v_scales = keep.tile([P, PASSES, V], U8, align_bytes=64)
        c_codes = keep.tile([P, PASSES, NC], U32, align_bytes=64)
        d_codes = keep.tile([P, PASSES, ND], U32, align_bytes=64)
        cs_early = keep.tile([P, EARLY, NC], U8, align_bytes=64)
        cs_mid = keep.tile([P, HP - EARLY, NC], U8, align_bytes=64)
        cs_late = keep.tile([P, HP, NC], U8, align_bytes=64)
        ds_early = keep.tile([P, HP, ND], U8, align_bytes=64)
        ds_late = keep.tile([P, HP, ND], U8, align_bytes=64)
        ax = keep.tile([P, JB, NC], BF16, align_bytes=64)
        ad = keep.tile([P, JB, ND], BF16, align_bytes=64)
        av = keep.tile([P, NC], BF16, align_bytes=64)
        gate_sb = keep.tile([P, JB, 2], BF16, align_bytes=64)
        gate_f = keep.tile([P, JB], F32, align_bytes=64)
        ox = keep.tile([P, JB, NC], F32, align_bytes=64)
        od = keep.tile([P, JB, ND], F32, align_bytes=64)
        ov = keep.tile([P, NC], F32, align_bytes=64)

        ctx.enter_context(tc.manual_schedule())

        nc.gpsimd.memset(cs_early[:].rearrange("p g n -> p (g n)").bitcast(I32), 0)
        nc.vector.memset(cs_mid[:].rearrange("p g n -> p (g n)").bitcast(I32), 0)
        nc.vector.memset(cs_late[:].rearrange("p g n -> p (g n)").bitcast(I32), 0)
        nc.vector.memset(ds_early[:].rearrange("p g n -> p (g n)").bitcast(I32), 0)
        nc.vector.memset(ds_late[:].rearrange("p g n -> p (g n)").bitcast(I32), 0)
        for q in range(4):
            nc.scalar.dma_start(
                out=cs_early[32 * q : 32 * q + 4, :, :].bitcast(I32), in_=cs_v[4 * q : 4 * q + 4, 0:EARLY, :]
            )
        for q in range(4):
            nc.gpsimd.dma_start(
                out=cs_late[32 * q : 32 * q + 4, :, :].bitcast(I32), in_=cs_v[4 * q : 4 * q + 4, HP:PASSES, :]
            )
        for q in range(4):
            nc.gpsimd.dma_start(
                out=ds_late[32 * q : 32 * q + 4, :, :].bitcast(I32), in_=ds_v[4 * q : 4 * q + 4, HP:PASSES, :]
            )
        with nc.allow_non_contiguous_dma(reason="one factor to a feature"):
            nc.scalar.dma_start(out=gate_sb[:, :, 0:1], in_=gate_v)

        def load_xc(s):
            nc.sync.dma_start(out=x_raw[:, s, :], in_=x_v[:, s, :])
            if s == 1:
                for q in range(4):
                    nc.sync.dma_start(
                        out=cs_mid[32 * q : 32 * q + 4, :, :].bitcast(I32), in_=cs_v[4 * q : 4 * q + 4, EARLY:HP, :]
                    )
            nc.sync.dma_start(out=c_codes[:, s, :].bitcast(I32), in_=c_v[:, s, :])

        def load_d(s0, s1):
            nc.sync.dma_start(out=d_codes[:, s0:s1, :].bitcast(I32), in_=d_v[:, s0:s1, :])

        def load_dirs(s0, s1):
            nc.sync.dma_start(out=v_raw[:, s0:s1, :], in_=dirs_v[:, s0:s1, :])

        for s in range(HP):
            load_xc(s)
        for q in range(4):
            nc.sync.dma_start(
                out=ds_early[32 * q : 32 * q + 4, :, :].bitcast(I32), in_=ds_v[4 * q : 4 * q + 4, 0:HP, :]
            )
        load_d(0, 2)
        load_d(2, 4)
        nc.sync.dma_start(out=ax[:], in_=acc_x_v)
        for s in range(HP, PASSES):
            load_xc(s)
        load_dirs(0, 4)
        load_d(4, 6)
        load_d(6, 8)
        load_dirs(4, 8)
        nc.sync.dma_start(out=ad[:], in_=acc_d_v)
        nc.sync.dma_start(out=av[:], in_=acc_v)

        def matmul(bank, codes, scales, rhs, rhs_scale, start, stop):
            nc.tensor.matmul_mx(
                out=bank[:],
                lhsT=codes.bitcast(E4M3),
                lhsT_scale=scales,
                rhs=rhs.bitcast(E5M2),
                rhs_scale=rhs_scale,
                start=start,
                stop=stop,
            )

        def c_scale(s, n0):
            if s < EARLY:
                return cs_early[:, s, n0 : n0 + NT]
            if s < HP:
                return cs_mid[:, s - EARLY, n0 : n0 + NT]
            return cs_late[:, s - HP, n0 : n0 + NT]

        def open_banks(numbers):
            banks = []
            for i in numbers:
                bank = psum.tile([P, NT], F32, name="bank%d" % i)
                banks.append(bank)
            return banks

        H = JB // 2

        def quantize_x(s):
            grouped = stage.tile([P, JB, P, PACK], BF16, align_bytes=64)
            raw = x_raw[:, s, :].rearrange("p (t j m) -> p j m t", t=PACK, j=JB)
            w = 1 if s == 0 else 2
            for b in range(0, H, w):
                nc.scalar.copy(out=grouped[:, H + b : H + b + w, :, :], in_=raw[:, H + b : H + b + w, :, :])
                nc.vector.tensor_copy(out=grouped[:, b : b + w, :, :], in_=raw[:, b : b + w, :, :])
            for b in range(0, JB, w):
                cols = slice(b * P, (b + w) * P)
                nc.vector.quantize_mx(
                    out=x_codes[:, s, cols].bitcast(E4M3),
                    scales=x_scales[:, s, cols],
                    in_=grouped[:, b : b + w, :, :].rearrange("p j m t -> p (j m t)"),
                )

        def x_times_c(s, banks, start, stop):
            for j in range(JB):
                for nh in range(2):
                    n0 = nh * NT
                    matmul(
                        banks[2 * j + nh],
                        x_codes[:, s, P * j : P * (j + 1)],
                        x_scales[:, s, P * j : P * (j + 1)],
                        c_codes[:, s, n0 : n0 + NT],
                        c_scale(s, n0),
                        start,
                        stop,
                    )

        def x_times_d(j, bank, passes):
            for s in passes:
                matmul(
                    bank,
                    x_codes[:, s, P * j : P * (j + 1)],
                    x_scales[:, s, P * j : P * (j + 1)],
                    d_codes[:, s, :],
                    ds_early[:, s, :] if s < HP else ds_late[:, s - HP, :],
                    s == passes[0],
                    s == passes[-1],
                )

        def add_xc(banks, addend, blocks, store):
            for j in blocks:
                for nh in range(2):
                    n0 = nh * NT
                    nc.vector.scalar_tensor_tensor(
                        out=ox[:, j, n0 : n0 + NT],
                        in0=banks[2 * j + nh][:],
                        scalar=gate_f[:, j : j + 1],
                        in1=addend[:, j, n0 : n0 + NT],
                        op0=MULT,
                        op1=ADD,
                    )
                if store and j % 2 == 1:
                    nc.sync.dma_start(out=out_x_v[:, j - 1 : j + 1, :], in_=ox[:, j - 1 : j + 1, :])

        xc = open_banks([0, 1, 2, 3, 4, 5, 6, 7])
        for s in range(HP):
            quantize_x(s)
            x_times_c(s, xc, s == 0, s == HP - 1)
        nc.vector.tensor_copy(out=gate_f[:], in_=gate_sb[:, :, 0])
        add_xc(xc, ax, range(H, JB), False)
        for j in range(H):
            for nh in range(2):
                nc.scalar.activation(
                    out=ox[:, j, nh * NT : (nh + 1) * NT],
                    in_=xc[2 * j + nh][:],
                    func=mybir.ActivationFunctionType.Copy,
                    scale=gate_f[:, j : j + 1],
                )
        xd = open_banks([0, 1, 2, 3])
        for j in range(JB):
            x_times_d(j, xd[j], range(0, HP))

        xc = open_banks([4, 5, 6, 7, 0, 1, 2, 3])
        for s in range(HP, PASSES):
            quantize_x(s)
            if s == HP:
                for j in range(JB):
                    nc.scalar.copy(out=od[:, j, :], in_=xd[j][:])
            j = s - HP - 1
            if 0 <= j < H:
                nc.vector.tensor_tensor(out=ox[:, j, :], in0=ox[:, j, :], in1=ax[:, j, :], op=ADD)
            x_times_c(s, xc, s == HP, s == PASSES - 1)
        add_xc(xc, ox, range(JB), True)
        xd = open_banks([4, 5, 6, 7])
        for j in range(JB):
            x_times_d(j, xd[j], range(HP, PASSES))

        for h in range(2):
            v_grouped = stage.tile([P, HP, V, PACK], BF16, align_bytes=64)
            s0, s1 = h * HP, (h + 1) * HP
            nc.scalar.copy(out=v_grouped[:], in_=v_raw[:, s0:s1, :].rearrange("p s (t c) -> p s c t", t=PACK))
            nc.vector.quantize_mx(
                out=v_codes[:, s0:s1, :].rearrange("p s c -> p (s c)").bitcast(E4M3),
                scales=v_scales[:, s0:s1, :].rearrange("p s c -> p (s c)"),
                in_=v_grouped[:].rearrange("p s c t -> p (s c t)"),
            )
            for j in range(2 * h, 2 * h + 2):
                nc.vector.tensor_tensor(out=od[:, j, :], in0=od[:, j, :], in1=ad[:, j, :], op=ADD)

        for j in range(JB):
            nc.vector.tensor_tensor(out=od[:, j, :], in0=xd[j][:], in1=od[:, j, :], op=ADD)
            if j % 2 == 1:
                nc.sync.dma_start(out=out_d_v[:, j - 1 : j + 1, :], in_=od[:, j - 1 : j + 1, :])

        for nh in range(2):
            n0 = nh * NT
            bank = open_banks([nh])[0]
            for s in range(PASSES):
                matmul(
                    bank,
                    v_codes[:, s, :],
                    v_scales[:, s, :],
                    c_codes[:, s, n0 : n0 + NT],
                    c_scale(s, n0),
                    s == 0,
                    s == PASSES - 1,
                )
            pieces = 1 + nh
            w = NT // pieces
            for i in range(pieces):
                cols = slice(n0 + i * w, n0 + (i + 1) * w)
                nc.vector.tensor_tensor(out=ov[:, cols], in0=bank[:, i * w : (i + 1) * w], in1=av[:, cols], op=ADD)
                nc.sync.dma_start(out=out_v[:, cols], in_=ov[:, cols])
